import numpy as np
import ml_dtypes


def mxq(x, axis, fmt="e4m3"):
    dtype, down = {"e4m3": (ml_dtypes.float8_e4m3fn, 7), "e5m2": (ml_dtypes.float8_e5m2, 14)}[fmt]
    v = np.moveaxis(np.asarray(x, np.float32).astype(ml_dtypes.bfloat16).astype(np.float64), axis, -1)
    blocks = v.reshape(v.shape[:-1] + (-1, 32))
    amax = np.abs(blocks).max(-1, keepdims=True)
    byte = np.maximum(np.where(amax > 0, np.frexp(amax)[1] - 1 + 127, 0) - down, 1)
    scale = np.exp2(byte - 127.0)
    codes = (blocks / scale).astype(np.float32).astype(dtype).astype(np.float64)
    return np.moveaxis((codes * scale).reshape(v.shape), -1, axis)


WIDE = False


def mx_kscale(k):
    if not WIDE:
        return np.ones(k)
    levels = np.array([10, -10, 5, -5, 0])
    if k % 512:
        return np.exp2(np.random.permutation(np.resize(levels, k // 32))).repeat(32)
    a = np.empty((k // 512, 16))
    for p in range(k // 512):
        a[p, :8] = np.random.permutation(np.resize(levels, 8))
        for g in range(8):
            far = levels[np.abs(levels - a[p, g]) >= 10]
            a[p, g + 8] = far[np.random.randint(len(far))]
    return np.exp2(a.ravel()).repeat(32)


def f64(x):
    return np.asarray(x).astype(np.float64)


def striped(idx):
    return np.tile(idx.reshape(-1, 16).T, (8, 1)).astype(np.uint16)


def unstriped(offs):
    return offs[:16].T.reshape(-1).astype(np.int64)


E2M1 = np.array([0.0, 0.5, 1.0, 1.5, 2.0, 3.0, 4.0, 6.0, -0.0, -0.5, -1.0, -1.5, -2.0, -3.0, -4.0, -6.0])


def pack_weight(w, fmt):
    k, n = w.shape
    w = f64(np.asarray(w, np.float32).astype(ml_dtypes.bfloat16)).reshape(k // 32, 32, n)
    amax = np.abs(w).max(1)
    if fmt == "e4m3":
        byte = np.frexp(amax)[1] - 1 + 127 - 7
    else:
        mant, ex = np.frexp(amax / 6.0)
        byte = np.where(mant > 0.5, ex, ex - 1) + 127
    byte = np.clip(np.where(amax > 0, byte, 1), 1, 254)
    scaled = (w * np.exp2(127.0 - byte)[:, None, :]).reshape(k, n).astype(np.float32)
    by_word = np.ascontiguousarray(scaled.reshape(k // 512, 128, 4, n).transpose(0, 1, 3, 2))
    if fmt == "e4m3":
        words = by_word.astype(ml_dtypes.float8_e4m3fn).view(np.uint8)
    else:
        c = by_word.astype(ml_dtypes.float4_e2m1fn).view(np.uint8) & 0xF
        words = (c[..., 0::2] | (c[..., 1::2] << 4)).reshape(k // 512, 128, 2 * n)
    return np.ascontiguousarray(words), np.ascontiguousarray(byte.astype(np.uint8).reshape(k // 512, 16, n))


def unpack_weight(words, scales, fmt):
    g, _, n = scales.shape
    words = np.ascontiguousarray(words).reshape(g, 128, n, -1)
    if fmt == "e4m3":
        vals = words.view(ml_dtypes.float8_e4m3fn).astype(np.float64)
    else:
        nib = np.empty((g, 128, n, 4), np.uint8)
        nib[..., 0::2] = words & 0xF
        nib[..., 1::2] = words >> 4
        vals = E2M1[nib]
    vals = vals * np.repeat(np.exp2(scales.astype(np.float64) - 127.0), 8, axis=1)[..., None]
    return vals.transpose(0, 1, 3, 2).reshape(g * 512, n)


def silu(v):
    return v / (1.0 + np.exp(-np.maximum(v, -700.0)))


G, K, M, T, S = 4, 512, 512, 2048, 256


def setup_inputs():
    n = np.random.standard_normal
    s = mx_kscale(K)[:, None]
    p_w4 = pack_weight(n((K, M)) / np.sqrt(K) / s, "e2m1")
    p_w8 = pack_weight(n((K, M)) / np.sqrt(K) / s, "e4m3")
    return {
        "xT": (n((K, T)) * s).astype(np.float32),
        "c": (n((K, S)) * s).astype(np.float32),
        "w4_words": p_w4[0],
        "w4_scales": p_w4[1],
        "w8_words": p_w8[0],
        "w8_scales": p_w8[1],
        "b": (0.3 * n(512)).astype(np.float32),
        "offs": striped(np.concatenate([np.random.permutation(T)[:S] for _ in range(G)])),
    }


def reference(xT, c, w4_words, w4_scales, w8_words, w8_scales, b, offs):
    idx = unstriped(offs).reshape(G, S)
    xm_ = mxq(np.max([f64(xT)[:, idx[g]] for g in range(G)], axis=0), 0, "e4m3")
    c_ = mxq(f64(c), 0, "e4m3")
    w4_ = unpack_weight(w4_words, w4_scales, "e2m1")
    w8_ = unpack_weight(w8_words, w8_scales, "e4m3")
    y = w4_.T @ xm_ + w8_.T @ c_
    return silu(y + f64(b)[:, None])

@@ -1,0 +1,134 @@
+from contextlib import ExitStack
+
+import concourse.mybir as mybir
+
+G, K, M, T, S = 4, 512, 512, 2048, 256
+FLOPS = 2 * 2 * K * M * S
+
+F32 = mybir.dt.float32
+BF16 = mybir.dt.bfloat16
+I32 = mybir.dt.int32
+U32 = mybir.dt.uint32
+U16 = mybir.dt.uint16
+U8 = mybir.dt.uint8
+FP8X4 = mybir.dt.float8_e4m3fn_x4
+FP4X4 = mybir.dt.float4_e2m1fn_x4
+MAX = mybir.AluOpType.max
+SILU = mybir.ActivationFunctionType.Silu
+
+P = 128
+PACK = 4
+HALF = 128
+CHUNKS = (((0, 256, 1024), (1024, 1344, 2048)), ((0, 512, 512), (512, 1024, 1024), (1024, 1280, 1536), (1536, 1696, 2048)))
+
+
+def tile_list_sage_silu_kernel(
+    tc, xT, c, w4_words, w4_scales, w8_words, w8_scales, b, offs, out
+):
+    nc = tc.nc
+    with ExitStack() as ctx:
+        keep = ctx.enter_context(tc.tile_pool(name="keep", bufs=1))
+        psum = ctx.enter_context(tc.psum_pool(name="psum", bufs=1))
+
+        offsets = keep.tile([P, G * S // 16], U16, name="offsets")
+        nc.sync.dma_start(offsets[:], offs)
+
+        w_scales = keep.tile([P, 2 * M], U8, name="w_scales", align_bytes=64)
+        nc.vector.memset(w_scales[:].bitcast(I32), 0)
+
+        x_rows = xT.rearrange("(p i) t -> p i t", i=PACK)
+        level = keep.tile([P, 2, 2, 2, 2 * HALF], BF16, name="level", align_bytes=64)
+
+        def load_scales(which, src, quads):
+            for q in quads:
+                nc.sync.dma_start(
+                    w_scales[32 * q : 32 * q + 4, which * M : (which + 1) * M].bitcast(I32),
+                    src[0, 4 * q : 4 * q + 4, :].bitcast(I32),
+                )
+
+        picked = []
+        for a in range(2):
+            window = keep.tile([P, T], U32, name="window%d" % a, align_bytes=64)
+            pairs = window[:].bitcast(BF16).rearrange("p (t e) -> p t e", e=2)
+            for n, (t0, tm, t1) in enumerate(CHUNKS[a]):
+                raw = keep.tile([P, 2, t1 - t0], F32, name="raw%d_%d" % (a, n), align_bytes=64)
+                nc.sync.dma_start(raw[:], x_rows[:, 2 * a : 2 * a + 2, t0:t1])
+                cols = raw[:].rearrange("p e t -> p t e")
+                if tm > t0:
+                    nc.scalar.copy(pairs[:, t0:tm, :], cols[:, 0 : tm - t0, :])
+                if t1 > tm:
+                    nc.vector.tensor_copy(pairs[:, tm:t1, :], cols[:, tm - t0 : t1 - t0, :])
+                if a == 0 and n == len(CHUNKS[0]) - 1:
+                    load_scales(0, w4_scales, range(4))
+                if a == 1 and n == 0:
+                    load_scales(1, w8_scales, range(4))
+            got = keep.tile([P, G * S], U32, name="got%d" % a, align_bytes=64)
+            nc.vector.tensor_copy(got[:], window[:].indirect(offsets[:]))
+            picked.append(got[:].bitcast(BF16).rearrange("p (u l h w) -> p u h l w", u=2, l=2, h=2))
+            if a == 0:
+                nc.vector.tensor_tensor(level[:, 0], picked[0][:, 0], picked[0][:, 1], MAX)
+
+        c_raw = keep.tile([P, PACK, S], F32, name="c_raw")
+        nc.sync.dma_start(c_raw[:], c.rearrange("(p i) j -> p i j", i=PACK))
+        w8 = keep.tile([P, M], U32, name="w8", align_bytes=64)
+        nc.sync.dma_start(w8[:].bitcast(I32), w8_words[0].rearrange("p n i -> p (n i)").bitcast(I32))
+        w4 = keep.tile([P, 2 * M], U8, name="w4", align_bytes=64)
+        nc.sync.dma_start(w4[:].bitcast(I32), w4_words[0].bitcast(I32))
+        bias = keep.tile([P, M // P], F32, name="bias")
+        with nc.allow_non_contiguous_dma(reason="one bias value for each output row"):
+            nc.sync.dma_start(bias[:], b.rearrange("(m p) -> p m", p=P))
+
+        c_cols = c_raw[:].rearrange("p i j -> p j i")
+        c_codes, c_scales = [], []
+        for h in range(2):
+            c_grouped = level[:, 1, h].rearrange("p l w -> p (l w)")
+            nc.scalar.copy(c_grouped.rearrange("p (j i) -> p j i", i=PACK), c_cols[:, h * HALF : (h + 1) * HALF, :])
+            c_codes.append(keep.tile([P, HALF], U32, name="c_codes%d" % h, align_bytes=64))
+            c_scales.append(keep.tile([P, HALF], U8, name="c_scales%d" % h, align_bytes=64))
+            nc.vector.quantize_mx(c_codes[h][:].bitcast(FP8X4), c_scales[h][:], c_grouped)
+
+        acc = {}
+        for h in range(2):
+            for m in range(M // P):
+                acc[h, m] = psum.tile([P, HALF], F32, name="acc%d_%d" % (h, m))
+                nc.tensor.matmul_mx(
+                    acc[h, m][:],
+                    lhsT=w8[:, m * P : (m + 1) * P].bitcast(FP8X4),
+                    lhsT_scale=w_scales[:, M + m * P : M + (m + 1) * P],
+                    rhs=c_codes[h][:].bitcast(FP8X4),
+                    rhs_scale=c_scales[h][:],
+                    start=True,
+                    stop=False,
+                )
+
+        for h in range(2):
+            nc.vector.tensor_tensor(level[:, 1, h], picked[1][:, 0, h], picked[1][:, 1, h], MAX)
+        xm = []
+        for h in range(2):
+            xm_h = keep.tile([P, HALF, 2, 2], BF16, name="xm%d" % h, align_bytes=64)
+            nc.vector.tensor_tensor(
+                xm_h[:],
+                level[:, :, h, 0, :].rearrange("p a (j e) -> p j a e", e=2),
+                level[:, :, h, 1, :].rearrange("p a (j e) -> p j a e", e=2),
+                MAX,
+            )
+            xm.append(xm_h)
+        rows_out = out.rearrange("(m p) j -> p m j", p=P)
+        for h in range(2):
+            cols = slice(h * HALF, (h + 1) * HALF)
+            codes = keep.tile([P, HALF], U32, name="xm_codes%d" % h, align_bytes=64)
+            scales = keep.tile([P, HALF], U8, name="xm_scales%d" % h, align_bytes=64)
+            nc.vector.quantize_mx(codes[:].bitcast(FP8X4), scales[:], xm[h][:].rearrange("p j a e -> p (j a e)"))
+            result = keep.tile([P, M // P, HALF], F32, name="result%d" % h)
+            for m in range(M // P):
+                nc.tensor.matmul_mx(
+                    acc[h, m][:],
+                    lhsT=w4[:, 2 * m * P : 2 * (m + 1) * P].bitcast(FP4X4),
+                    lhsT_scale=w_scales[:, m * P : (m + 1) * P],
+                    rhs=codes[:].bitcast(FP8X4),
+                    rhs_scale=scales[:],
+                    start=False,
+                    stop=True,
+                )
+                nc.scalar.activation(result[:, m, :], acc[h, m][:], SILU, bias=bias[:, m : m + 1])
+            nc.sync.dma_start(rows_out[:, :, cols], result[:])

@@ -19,7 +19,7 @@ SILU = mybir.ActivationFunctionType.Silu
 P = 128
 PACK = 4
 HALF = 128
-CHUNKS = (((0, 256, 1024), (1024, 1344, 2048)), ((0, 512, 512), (512, 1024, 1024), (1024, 1280, 1536), (1536, 1696, 2048)))
+CHUNKS = (((0, 1024, 1024), (1024, 1344, 2048)), ((0, 512, 512), (512, 1024, 1024), (1024, 1280, 1536), (1536, 1696, 2048)))
 
 
 def tile_list_sage_silu_kernel(
@@ -34,18 +34,23 @@ def tile_list_sage_silu_kernel(
         nc.sync.dma_start(offsets[:], offs)
 
         w_scales = keep.tile([P, 2 * M], U8, name="w_scales", align_bytes=64)
-        nc.vector.memset(w_scales[:].bitcast(I32), 0)
+        nc.gpsimd.memset(w_scales[:].bitcast(I32), 0)
+        warm = keep.tile([P, 8], F32, name="warm")
+        nc.vector.memset(warm[:, 0:1], 0.0)
+        nc.scalar.activation(warm[:, 4:5], warm[:, 0:1], SILU)
 
         x_rows = xT.rearrange("(p i) t -> p i t", i=PACK)
         level = keep.tile([P, 2, 2, 2, 2 * HALF], BF16, name="level", align_bytes=64)
 
         def load_scales(which, src, quads):
             for q in quads:
-                nc.sync.dma_start(
+                nc.gpsimd.dma_start(
                     w_scales[32 * q : 32 * q + 4, which * M : (which + 1) * M].bitcast(I32),
                     src[0, 4 * q : 4 * q + 4, :].bitcast(I32),
                 )
 
+        load_scales(1, w8_scales, range(4))
+        load_scales(0, w4_scales, range(4))
         picked = []
         for a in range(2):
             window = keep.tile([P, T], U32, name="window%d" % a, align_bytes=64)
@@ -58,10 +63,6 @@ def tile_list_sage_silu_kernel(
                     nc.scalar.copy(pairs[:, t0:tm, :], cols[:, 0 : tm - t0, :])
                 if t1 > tm:
                     nc.vector.tensor_copy(pairs[:, tm:t1, :], cols[:, tm - t0 : t1 - t0, :])
-                if a == 0 and n == len(CHUNKS[0]) - 1:
-                    load_scales(0, w4_scales, range(4))
-                if a == 1 and n == 0:
-                    load_scales(1, w8_scales, range(4))
             got = keep.tile([P, G * S], U32, name="got%d" % a, align_bytes=64)
             nc.vector.tensor_copy(got[:], window[:].indirect(offsets[:]))
             picked.append(got[:].bitcast(BF16).rearrange("p (u l h w) -> p u h l w", u=2, l=2, h=2))
@@ -131,4 +132,5 @@ def tile_list_sage_silu_kernel(
                     stop=True,
                 )
                 nc.scalar.activation(result[:, m, :], acc[h, m][:], SILU, bias=bias[:, m : m + 1])
-            nc.sync.dma_start(rows_out[:, :, cols], result[:])
+                if m % 2 == 1:
+                    nc.sync.dma_start(rows_out[:, m - 1 : m + 1, cols], result[:, m - 1 : m + 1, :])

@@ -1,6 +1,7 @@
 from contextlib import ExitStack
 
 import concourse.mybir as mybir
+from concourse.masks import make_identity
 
 G, K, M, T, S = 4, 512, 512, 2048, 256
 FLOPS = 2 * 2 * K * M * S
@@ -19,7 +20,13 @@ SILU = mybir.ActivationFunctionType.Silu
 P = 128
 PACK = 4
 HALF = 128
-CHUNKS = (((0, 1024, 1024), (1024, 1344, 2048)), ((0, 512, 512), (512, 1024, 1024), (1024, 1280, 1536), (1536, 1696, 2048)))
+TILES = M // P
+CHUNKS = (((0, 512, 1536), (1536, 1696, 2048)), ((0, 640, 1024), (1024, 1216, 1664), (1664, 1792, 2048)))
+
+
+def load_scale_rows(engine, plane, src):
+    for q in range(4):
+        engine.dma_start(plane[32 * q : 32 * q + 4, :].bitcast(I32), src[0, 4 * q : 4 * q + 4, :].bitcast(I32))
 
 
 def tile_list_sage_silu_kernel(
@@ -31,26 +38,22 @@ def tile_list_sage_silu_kernel(
         psum = ctx.enter_context(tc.psum_pool(name="psum", bufs=1))
 
         offsets = keep.tile([P, G * S // 16], U16, name="offsets")
-        nc.sync.dma_start(offsets[:], offs)
 
-        w_scales = keep.tile([P, 2 * M], U8, name="w_scales", align_bytes=64)
-        nc.gpsimd.memset(w_scales[:].bitcast(I32), 0)
         warm = keep.tile([P, 8], F32, name="warm")
         nc.vector.memset(warm[:, 0:1], 0.0)
         nc.scalar.activation(warm[:, 4:5], warm[:, 0:1], SILU)
+        b_rows = keep.tile([P, P], F32, name="b_rows")
+        nc.gpsimd.memset(b_rows[:], 0.0)
+        w_scales = keep.tile([P, 2 * M], U8, name="w_scales", align_bytes=64)
+        nc.vector.memset(w_scales[:].bitcast(I32), 0)
+        identity = keep.tile([P, P], F32, name="identity")
+        make_identity(nc, identity[:])
+
+        load_scale_rows(nc.gpsimd, w_scales[:, M : 2 * M], w8_scales)
 
         x_rows = xT.rearrange("(p i) t -> p i t", i=PACK)
         level = keep.tile([P, 2, 2, 2, 2 * HALF], BF16, name="level", align_bytes=64)
 
-        def load_scales(which, src, quads):
-            for q in quads:
-                nc.gpsimd.dma_start(
-                    w_scales[32 * q : 32 * q + 4, which * M : (which + 1) * M].bitcast(I32),
-                    src[0, 4 * q : 4 * q + 4, :].bitcast(I32),
-                )
-
-        load_scales(1, w8_scales, range(4))
-        load_scales(0, w4_scales, range(4))
         picked = []
         for a in range(2):
             window = keep.tile([P, T], U32, name="window%d" % a, align_bytes=64)
@@ -58,6 +61,10 @@ def tile_list_sage_silu_kernel(
             for n, (t0, tm, t1) in enumerate(CHUNKS[a]):
                 raw = keep.tile([P, 2, t1 - t0], F32, name="raw%d_%d" % (a, n), align_bytes=64)
                 nc.sync.dma_start(raw[:], x_rows[:, 2 * a : 2 * a + 2, t0:t1])
+                if (a, n) == (0, 0):
+                    nc.sync.dma_start(offsets[:], offs)
+                if (a, n) == (0, 1):
+                    nc.sync.dma_start(b_rows[0:TILES, :], b.rearrange("(m p) -> m p", p=P))
                 cols = raw[:].rearrange("p e t -> p t e")
                 if tm > t0:
                     nc.scalar.copy(pairs[:, t0:tm, :], cols[:, 0 : tm - t0, :])
@@ -67,31 +74,39 @@ def tile_list_sage_silu_kernel(
             nc.vector.tensor_copy(got[:], window[:].indirect(offsets[:]))
             picked.append(got[:].bitcast(BF16).rearrange("p (u l h w) -> p u h l w", u=2, l=2, h=2))
             if a == 0:
-                nc.vector.tensor_tensor(level[:, 0], picked[0][:, 0], picked[0][:, 1], MAX)
+                nc.vector.tensor_tensor(
+                    level[:, :, 0].rearrange("p h l w -> p l h w"),
+                    picked[0][:, 0].rearrange("p h l w -> p l h w"),
+                    picked[0][:, 1].rearrange("p h l w -> p l h w"),
+                    MAX,
+                )
 
+        b_turned = psum.tile([P, P], F32, tag="acc1_3", name="b_turned")
+        nc.tensor.transpose(b_turned[:], b_rows[:], identity[:])
+        bias = keep.tile([P, TILES], F32, name="bias")
+        nc.scalar.copy(bias[:], b_turned[:, 0:TILES])
         c_raw = keep.tile([P, PACK, S], F32, name="c_raw")
         nc.sync.dma_start(c_raw[:], c.rearrange("(p i) j -> p i j", i=PACK))
         w8 = keep.tile([P, M], U32, name="w8", align_bytes=64)
         nc.sync.dma_start(w8[:].bitcast(I32), w8_words[0].rearrange("p n i -> p (n i)").bitcast(I32))
         w4 = keep.tile([P, 2 * M], U8, name="w4", align_bytes=64)
         nc.sync.dma_start(w4[:].bitcast(I32), w4_words[0].bitcast(I32))
-        bias = keep.tile([P, M // P], F32, name="bias")
-        with nc.allow_non_contiguous_dma(reason="one bias value for each output row"):
-            nc.sync.dma_start(bias[:], b.rearrange("(m p) -> p m", p=P))
+        load_scale_rows(nc.sync, w_scales[:, 0:M], w4_scales)
 
-        c_cols = c_raw[:].rearrange("p i j -> p j i")
+        c_grouped = level[:, :, 1].rearrange("p h l w -> p h (l w)")
+        nc.scalar.copy(
+            c_grouped.rearrange("p h (j i) -> p h j i", i=PACK), c_raw[:].rearrange("p i (h j) -> p h j i", h=2)
+        )
         c_codes, c_scales = [], []
         for h in range(2):
-            c_grouped = level[:, 1, h].rearrange("p l w -> p (l w)")
-            nc.scalar.copy(c_grouped.rearrange("p (j i) -> p j i", i=PACK), c_cols[:, h * HALF : (h + 1) * HALF, :])
             c_codes.append(keep.tile([P, HALF], U32, name="c_codes%d" % h, align_bytes=64))
             c_scales.append(keep.tile([P, HALF], U8, name="c_scales%d" % h, align_bytes=64))
-            nc.vector.quantize_mx(c_codes[h][:].bitcast(FP8X4), c_scales[h][:], c_grouped)
+            nc.vector.quantize_mx(c_codes[h][:].bitcast(FP8X4), c_scales[h][:], c_grouped[:, h, :])
 
         acc = {}
         for h in range(2):
-            for m in range(M // P):
-                acc[h, m] = psum.tile([P, HALF], F32, name="acc%d_%d" % (h, m))
+            for m in range(TILES):
+                acc[h, m] = psum.tile([P, HALF], F32, tag="acc%d_%d" % (h, m), name="acc%d_%d" % (h, m))
                 nc.tensor.matmul_mx(
                     acc[h, m][:],
                     lhsT=w8[:, m * P : (m + 1) * P].bitcast(FP8X4),
@@ -103,14 +118,14 @@ def tile_list_sage_silu_kernel(
                 )
 
         for h in range(2):
-            nc.vector.tensor_tensor(level[:, 1, h], picked[1][:, 0, h], picked[1][:, 1, h], MAX)
+            nc.vector.tensor_tensor(level[:, h, 1], picked[1][:, 0, h], picked[1][:, 1, h], MAX)
         xm = []
         for h in range(2):
             xm_h = keep.tile([P, HALF, 2, 2], BF16, name="xm%d" % h, align_bytes=64)
             nc.vector.tensor_tensor(
                 xm_h[:],
-                level[:, :, h, 0, :].rearrange("p a (j e) -> p j a e", e=2),
-                level[:, :, h, 1, :].rearrange("p a (j e) -> p j a e", e=2),
+                level[:, h, :, 0, :].rearrange("p a (j e) -> p j a e", e=2),
+                level[:, h, :, 1, :].rearrange("p a (j e) -> p j a e", e=2),
                 MAX,
             )
             xm.append(xm_h)
@@ -120,8 +135,8 @@ def tile_list_sage_silu_kernel(
             codes = keep.tile([P, HALF], U32, name="xm_codes%d" % h, align_bytes=64)
             scales = keep.tile([P, HALF], U8, name="xm_scales%d" % h, align_bytes=64)
             nc.vector.quantize_mx(codes[:].bitcast(FP8X4), scales[:], xm[h][:].rearrange("p j a e -> p (j a e)"))
-            result = keep.tile([P, M // P, HALF], F32, name="result%d" % h)
-            for m in range(M // P):
+            result = keep.tile([P, TILES, HALF], F32, name="result%d" % h)
+            for m in range(TILES):
                 nc.tensor.matmul_mx(
                     acc[h, m][:],
                     lhsT=w4[:, 2 * m * P : 2 * (m + 1) * P].bitcast(FP4X4),

@@ -21,7 +21,8 @@ P = 128
 PACK = 4
 HALF = 128
 TILES = M // P
-CHUNKS = (((0, 512, 1536), (1536, 1696, 2048)), ((0, 640, 1024), (1024, 1216, 1664), (1664, 1792, 2048)))
+STORES = (((0, 2), (2, 4)), ((0, 2), (2, 3), (3, 4)))
+CHUNKS = (((0, 480, 1408), (1408, 1616, 2048)), ((0, 768, 768), (768, 1088, 1664), (1664, 1792, 2048)))
 
 
 def load_scale_rows(engine, plane, src):
@@ -75,7 +76,7 @@ def tile_list_sage_silu_kernel(
             picked.append(got[:].bitcast(BF16).rearrange("p (u l h w) -> p u h l w", u=2, l=2, h=2))
             if a == 0:
                 nc.vector.tensor_tensor(
-                    level[:, :, 0].rearrange("p h l w -> p l h w"),
+                    level[:, 0].rearrange("p h l w -> p l h w"),
                     picked[0][:, 0].rearrange("p h l w -> p l h w"),
                     picked[0][:, 1].rearrange("p h l w -> p l h w"),
                     MAX,
@@ -93,9 +94,10 @@ def tile_list_sage_silu_kernel(
         nc.sync.dma_start(w4[:].bitcast(I32), w4_words[0].bitcast(I32))
         load_scale_rows(nc.sync, w_scales[:, 0:M], w4_scales)
 
-        c_grouped = level[:, :, 1].rearrange("p h l w -> p h (l w)")
+        c_grouped = level[:, 1].rearrange("p h l w -> p h (l w)")
         nc.scalar.copy(
-            c_grouped.rearrange("p h (j i) -> p h j i", i=PACK), c_raw[:].rearrange("p i (h j) -> p h j i", h=2)
+            c_grouped.rearrange("p h (q r i) -> p (h q) i r", r=4, i=PACK),
+            c_raw[:].rearrange("p i (q r) -> p q i r", r=4),
         )
         c_codes, c_scales = [], []
         for h in range(2):
@@ -118,14 +120,14 @@ def tile_list_sage_silu_kernel(
                 )
 
         for h in range(2):
-            nc.vector.tensor_tensor(level[:, h, 1], picked[1][:, 0, h], picked[1][:, 1, h], MAX)
+            nc.vector.tensor_tensor(level[:, 1, h], picked[1][:, 0, h], picked[1][:, 1, h], MAX)
         xm = []
         for h in range(2):
             xm_h = keep.tile([P, HALF, 2, 2], BF16, name="xm%d" % h, align_bytes=64)
             nc.vector.tensor_tensor(
                 xm_h[:],
-                level[:, h, :, 0, :].rearrange("p a (j e) -> p j a e", e=2),
-                level[:, h, :, 1, :].rearrange("p a (j e) -> p j a e", e=2),
+                level[:, :, h, 0, :].rearrange("p a (j e) -> p j a e", e=2),
+                level[:, :, h, 1, :].rearrange("p a (j e) -> p j a e", e=2),
                 MAX,
             )
             xm.append(xm_h)
@@ -147,5 +149,6 @@ def tile_list_sage_silu_kernel(
                     stop=True,
                 )
                 nc.scalar.activation(result[:, m, :], acc[h, m][:], SILU, bias=bias[:, m : m + 1])
-                if m % 2 == 1:
-                    nc.sync.dma_start(rows_out[:, m - 1 : m + 1, cols], result[:, m - 1 : m + 1, :])
+                for m0, m1 in STORES[h]:
+                    if m1 == m + 1:
+                        nc.sync.dma_start(rows_out[:, m0:m1, cols], result[:, m0:m1, :])

@@ -40,9 +40,6 @@ def tile_list_sage_silu_kernel(
 
         offsets = keep.tile([P, G * S // 16], U16, name="offsets")
 
-        warm = keep.tile([P, 8], F32, name="warm")
-        nc.vector.memset(warm[:, 0:1], 0.0)
-        nc.scalar.activation(warm[:, 4:5], warm[:, 0:1], SILU)
         b_rows = keep.tile([P, P], F32, name="b_rows")
         nc.gpsimd.memset(b_rows[:], 0.0)
         w_scales = keep.tile([P, 2 * M], U8, name="w_scales", align_bytes=64)

from contextlib import ExitStack

import concourse.mybir as mybir
from concourse.masks import make_identity

G, K, M, T, S = 4, 512, 512, 2048, 256
FLOPS = 2 * 2 * K * M * S

F32 = mybir.dt.float32
BF16 = mybir.dt.bfloat16
I32 = mybir.dt.int32
U32 = mybir.dt.uint32
U16 = mybir.dt.uint16
U8 = mybir.dt.uint8
FP8X4 = mybir.dt.float8_e4m3fn_x4
FP4X4 = mybir.dt.float4_e2m1fn_x4
MAX = mybir.AluOpType.max
SILU = mybir.ActivationFunctionType.Silu

P = 128
PACK = 4
HALF = 128
TILES = M // P
STORES = (((0, 2), (2, 4)), ((0, 2), (2, 3), (3, 4)))
CHUNKS = (((0, 480, 1408), (1408, 1616, 2048)), ((0, 768, 768), (768, 1088, 1664), (1664, 1792, 2048)))


def load_scale_rows(engine, plane, src):
    for q in range(4):
        engine.dma_start(plane[32 * q : 32 * q + 4, :].bitcast(I32), src[0, 4 * q : 4 * q + 4, :].bitcast(I32))


def tile_list_sage_silu_kernel(
    tc, xT, c, w4_words, w4_scales, w8_words, w8_scales, b, offs, out
):
    nc = tc.nc
    with ExitStack() as ctx:
        keep = ctx.enter_context(tc.tile_pool(name="keep", bufs=1))
        psum = ctx.enter_context(tc.psum_pool(name="psum", bufs=1))

        offsets = keep.tile([P, G * S // 16], U16, name="offsets")

        b_rows = keep.tile([P, P], F32, name="b_rows")
        nc.gpsimd.memset(b_rows[:], 0.0)
        w_scales = keep.tile([P, 2 * M], U8, name="w_scales", align_bytes=64)
        nc.vector.memset(w_scales[:].bitcast(I32), 0)
        identity = keep.tile([P, P], F32, name="identity")
        make_identity(nc, identity[:])

        load_scale_rows(nc.gpsimd, w_scales[:, M : 2 * M], w8_scales)

        x_rows = xT.rearrange("(p i) t -> p i t", i=PACK)
        level = keep.tile([P, 2, 2, 2, 2 * HALF], BF16, name="level", align_bytes=64)

        picked = []
        for a in range(2):
            window = keep.tile([P, T], U32, name="window%d" % a, align_bytes=64)
            pairs = window[:].bitcast(BF16).rearrange("p (t e) -> p t e", e=2)
            for n, (t0, tm, t1) in enumerate(CHUNKS[a]):
                raw = keep.tile([P, 2, t1 - t0], F32, name="raw%d_%d" % (a, n), align_bytes=64)
                nc.sync.dma_start(raw[:], x_rows[:, 2 * a : 2 * a + 2, t0:t1])
                if (a, n) == (0, 0):
                    nc.sync.dma_start(offsets[:], offs)
                if (a, n) == (0, 1):
                    nc.sync.dma_start(b_rows[0:TILES, :], b.rearrange("(m p) -> m p", p=P))
                cols = raw[:].rearrange("p e t -> p t e")
                if tm > t0:
                    nc.scalar.copy(pairs[:, t0:tm, :], cols[:, 0 : tm - t0, :])
                if t1 > tm:
                    nc.vector.tensor_copy(pairs[:, tm:t1, :], cols[:, tm - t0 : t1 - t0, :])
            got = keep.tile([P, G * S], U32, name="got%d" % a, align_bytes=64)
            nc.vector.tensor_copy(got[:], window[:].indirect(offsets[:]))
            picked.append(got[:].bitcast(BF16).rearrange("p (u l h w) -> p u h l w", u=2, l=2, h=2))
            if a == 0:
                nc.vector.tensor_tensor(
                    level[:, 0].rearrange("p h l w -> p l h w"),
                    picked[0][:, 0].rearrange("p h l w -> p l h w"),
                    picked[0][:, 1].rearrange("p h l w -> p l h w"),
                    MAX,
                )

        b_turned = psum.tile([P, P], F32, tag="acc1_3", name="b_turned")
        nc.tensor.transpose(b_turned[:], b_rows[:], identity[:])
        bias = keep.tile([P, TILES], F32, name="bias")
        nc.scalar.copy(bias[:], b_turned[:, 0:TILES])
        c_raw = keep.tile([P, PACK, S], F32, name="c_raw")
        nc.sync.dma_start(c_raw[:], c.rearrange("(p i) j -> p i j", i=PACK))
        w8 = keep.tile([P, M], U32, name="w8", align_bytes=64)
        nc.sync.dma_start(w8[:].bitcast(I32), w8_words[0].rearrange("p n i -> p (n i)").bitcast(I32))
        w4 = keep.tile([P, 2 * M], U8, name="w4", align_bytes=64)
        nc.sync.dma_start(w4[:].bitcast(I32), w4_words[0].bitcast(I32))
        load_scale_rows(nc.sync, w_scales[:, 0:M], w4_scales)

        c_grouped = level[:, 1].rearrange("p h l w -> p h (l w)")
        nc.scalar.copy(
            c_grouped.rearrange("p h (q r i) -> p (h q) i r", r=4, i=PACK),
            c_raw[:].rearrange("p i (q r) -> p q i r", r=4),
        )
        c_codes, c_scales = [], []
        for h in range(2):
            c_codes.append(keep.tile([P, HALF], U32, name="c_codes%d" % h, align_bytes=64))
            c_scales.append(keep.tile([P, HALF], U8, name="c_scales%d" % h, align_bytes=64))
            nc.vector.quantize_mx(c_codes[h][:].bitcast(FP8X4), c_scales[h][:], c_grouped[:, h, :])

        acc = {}
        for h in range(2):
            for m in range(TILES):
                acc[h, m] = psum.tile([P, HALF], F32, tag="acc%d_%d" % (h, m), name="acc%d_%d" % (h, m))
                nc.tensor.matmul_mx(
                    acc[h, m][:],
                    lhsT=w8[:, m * P : (m + 1) * P].bitcast(FP8X4),
                    lhsT_scale=w_scales[:, M + m * P : M + (m + 1) * P],
                    rhs=c_codes[h][:].bitcast(FP8X4),
                    rhs_scale=c_scales[h][:],
                    start=True,
                    stop=False,
                )

        for h in range(2):
            nc.vector.tensor_tensor(level[:, 1, h], picked[1][:, 0, h], picked[1][:, 1, h], MAX)
        xm = []
        for h in range(2):
            xm_h = keep.tile([P, HALF, 2, 2], BF16, name="xm%d" % h, align_bytes=64)
            nc.vector.tensor_tensor(
                xm_h[:],
                level[:, :, h, 0, :].rearrange("p a (j e) -> p j a e", e=2),
                level[:, :, h, 1, :].rearrange("p a (j e) -> p j a e", e=2),
                MAX,
            )
            xm.append(xm_h)
        rows_out = out.rearrange("(m p) j -> p m j", p=P)
        for h in range(2):
            cols = slice(h * HALF, (h + 1) * HALF)
            codes = keep.tile([P, HALF], U32, name="xm_codes%d" % h, align_bytes=64)
            scales = keep.tile([P, HALF], U8, name="xm_scales%d" % h, align_bytes=64)
            nc.vector.quantize_mx(codes[:].bitcast(FP8X4), scales[:], xm[h][:].rearrange("p j a e -> p (j a e)"))
            result = keep.tile([P, TILES, HALF], F32, name="result%d" % h)
            for m in range(TILES):
                nc.tensor.matmul_mx(
                    acc[h, m][:],
                    lhsT=w4[:, 2 * m * P : 2 * (m + 1) * P].bitcast(FP4X4),
                    lhsT_scale=w_scales[:, m * P : (m + 1) * P],
                    rhs=codes[:].bitcast(FP8X4),
                    rhs_scale=scales[:],
                    start=False,
                    stop=True,
                )
                nc.scalar.activation(result[:, m, :], acc[h, m][:], SILU, bias=bias[:, m : m + 1])
                for m0, m1 in STORES[h]:
                    if m1 == m + 1:
                        nc.sync.dma_start(rows_out[:, m0:m1, cols], result[:, m0:m1, :])
